import numpy as np
import ml_dtypes


def mxq(x, axis, fmt="e4m3"):
    dtype, down = {"e4m3": (ml_dtypes.float8_e4m3fn, 7), "e5m2": (ml_dtypes.float8_e5m2, 14)}[fmt]
    v = np.moveaxis(np.asarray(x, np.float32).astype(ml_dtypes.bfloat16).astype(np.float64), axis, -1)
    blocks = v.reshape(v.shape[:-1] + (-1, 32))
    amax = np.abs(blocks).max(-1, keepdims=True)
    byte = np.maximum(np.where(amax > 0, np.frexp(amax)[1] - 1 + 127, 0) - down, 1)
    scale = np.exp2(byte - 127.0)
    codes = (blocks / scale).astype(np.float32).astype(dtype).astype(np.float64)
    return np.moveaxis((codes * scale).reshape(v.shape), -1, axis)


WIDE = False


def mx_kscale(k):
    if not WIDE:
        return np.ones(k)
    levels = np.array([10, -10, 5, -5, 0])
    if k % 512:
        return np.exp2(np.random.permutation(np.resize(levels, k // 32))).repeat(32)
    a = np.empty((k // 512, 16))
    for p in range(k // 512):
        a[p, :8] = np.random.permutation(np.resize(levels, 8))
        for g in range(8):
            far = levels[np.abs(levels - a[p, g]) >= 10]
            a[p, g + 8] = far[np.random.randint(len(far))]
    return np.exp2(a.ravel()).repeat(32)


def f64(x):
    return np.asarray(x).astype(np.float64)


E2M1 = np.array([0.0, 0.5, 1.0, 1.5, 2.0, 3.0, 4.0, 6.0, -0.0, -0.5, -1.0, -1.5, -2.0, -3.0, -4.0, -6.0])


def pack_weight(w, fmt):
    k, n = w.shape
    w = f64(np.asarray(w, np.float32).astype(ml_dtypes.bfloat16)).reshape(k // 32, 32, n)
    amax = np.abs(w).max(1)
    if fmt == "e4m3":
        byte = np.frexp(amax)[1] - 1 + 127 - 7
    else:
        mant, ex = np.frexp(amax / 6.0)
        byte = np.where(mant > 0.5, ex, ex - 1) + 127
    byte = np.clip(np.where(amax > 0, byte, 1), 1, 254)
    scaled = (w * np.exp2(127.0 - byte)[:, None, :]).reshape(k, n).astype(np.float32)
    by_word = np.ascontiguousarray(scaled.reshape(k // 512, 128, 4, n).transpose(0, 1, 3, 2))
    if fmt == "e4m3":
        words = by_word.astype(ml_dtypes.float8_e4m3fn).view(np.uint8)
    else:
        c = by_word.astype(ml_dtypes.float4_e2m1fn).view(np.uint8) & 0xF
        words = (c[..., 0::2] | (c[..., 1::2] << 4)).reshape(k // 512, 128, 2 * n)
    return np.ascontiguousarray(words), np.ascontiguousarray(byte.astype(np.uint8).reshape(k // 512, 16, n))


def unpack_weight(words, scales, fmt):
    g, _, n = scales.shape
    words = np.ascontiguousarray(words).reshape(g, 128, n, -1)
    if fmt == "e4m3":
        vals = words.view(ml_dtypes.float8_e4m3fn).astype(np.float64)
    else:
        nib = np.empty((g, 128, n, 4), np.uint8)
        nib[..., 0::2] = words & 0xF
        nib[..., 1::2] = words >> 4
        vals = E2M1[nib]
    vals = vals * np.repeat(np.exp2(scales.astype(np.float64) - 127.0), 8, axis=1)[..., None]
    return vals.transpose(0, 1, 3, 2).reshape(g * 512, n)


def silu(v):
    return v / (1.0 + np.exp(-np.maximum(v, -700.0)))


K, M, T = 1536, 1024, 1536


def setup_inputs():
    n = np.random.standard_normal
    s = mx_kscale(K)[:, None]
    w = n((K, M)) / np.sqrt(K) / s
    w4 = pack_weight(w, "e2m1")
    rest = w - unpack_weight(*w4, "e2m1")
    p_r8 = pack_weight(rest, "e4m3")
    return {
        "x": (n((K, T)) * s).astype(np.float32),
        "w4_words": w4[0],
        "w4_scales": w4[1],
        "r8_words": p_r8[0],
        "r8_scales": p_r8[1],
        "b": (0.3 * n(1024)).astype(np.float32),
    }


def reference(x, w4_words, w4_scales, r8_words, r8_scales, b):
    x_ = mxq(f64(x), 0, "e4m3")
    w4_ = unpack_weight(w4_words, w4_scales, "e2m1")
    r8_ = unpack_weight(r8_words, r8_scales, "e4m3")
    y = w4_.T @ x_ + r8_.T @ x_
    return silu(y + f64(b)[:, None])

@@ -1,0 +1,193 @@
+from contextlib import ExitStack
+
+import concourse.mybir as mybir
+
+K, M, T = 1536, 1024, 1536
+FLOPS = 2 * 2 * K * M * T
+
+F32 = mybir.dt.float32
+BF16 = mybir.dt.bfloat16
+I32 = mybir.dt.int32
+U32 = mybir.dt.uint32
+U8 = mybir.dt.uint8
+FP8X4 = mybir.dt.float8_e4m3fn_x4
+FP4X4 = mybir.dt.float4_e2m1fn_x4
+ACT = mybir.ActivationFunctionType
+
+P = 128
+PACK = 4
+G = K // 512
+MT = M // 128
+TW = 512
+NT = T // TW
+HALF = 256
+V_COLS = 160
+
+
+def tile_mix_resid_fm_silu_kernel(tc, x, w4_words, w4_scales, r8_words, r8_scales, b, out):
+    nc = tc.nc
+    with ExitStack() as ctx:
+        keep = ctx.enter_context(tc.tile_pool(name="keep", bufs=1))
+        stage = ctx.enter_context(tc.tile_pool(name="stage", bufs=6))
+        outs = ctx.enter_context(tc.tile_pool(name="outs", bufs=26))
+        psum = ctx.enter_context(tc.psum_pool(name="psum", bufs=1))
+        ctx.enter_context(tc.manual_schedule())
+
+        raw = {}
+        codes = {}
+        planes = {}
+        for t in range(NT):
+            for g in range(G):
+                raw[g, t] = keep.tile([P, PACK, TW], F32, name="raw_%d_%d" % (g, t), align_bytes=64)
+                codes[g, t] = keep.tile([P, TW], U32, name="codes_%d_%d" % (g, t), align_bytes=256)
+                planes[g, t] = keep.tile([P, TW], U8, name="plane_%d_%d" % (g, t), align_bytes=256)
+        w4 = [keep.tile([P, 2 * M], U8, name="w4_%d" % g, align_bytes=256) for g in range(G)]
+        r8 = [keep.tile([P, 4 * M], U8, name="r8_%d" % g, align_bytes=256) for g in range(G)]
+        w4s = keep.tile([P, G, M], U8, name="w4s", align_bytes=256)
+        r8s = keep.tile([P, G, M], U8, name="r8s", align_bytes=256)
+        b_rows = keep.tile([P, 32], F32, name="b_rows", align_bytes=64)
+        b_cols = keep.tile([P, 32], F32, name="b_cols", align_bytes=64)
+        warm = keep.tile([P, 1], F32, name="warm")
+        warm_out = keep.tile([P, 1], F32, name="warm_out")
+
+        w4s_i = w4s[:].rearrange("p g n -> p (g n)").bitcast(I32)
+        r8s_i = r8s[:].rearrange("p g n -> p (g n)").bitcast(I32)
+        nc.vector.memset(w4s_i, 0)
+        nc.vector.memset(warm[:], 0.0)
+        nc.gpsimd.memset(b_rows[:], 0.0)
+        nc.vector.memset(r8s_i, 0)
+
+        def load_x(g, t, c0, c1):
+            nc.sync.dma_start(
+                out=raw[g, t][:, :, c0:c1],
+                in_=x[512 * g : 512 * (g + 1), TW * t + c0 : TW * t + c1].rearrange("(p j) t -> p j t", j=PACK),
+            )
+
+        def load_w4(g):
+            nc.sync.dma_start(out=w4[g][:].bitcast(I32), in_=w4_words[g].bitcast(I32))
+
+        def load_r8(g):
+            nc.sync.dma_start(out=r8[g][:].bitcast(I32), in_=r8_words[g].rearrange("p n i -> p (n i)").bitcast(I32))
+
+        load_x(0, 0, 0, HALF)
+        load_x(0, 0, HALF, TW)
+        def load_scales(view, scales):
+            rows = scales.bitcast(I32).rearrange("g (q r) n -> r q g n", r=4)
+            for r in range(4):
+                nc.sync.dma_start(out=view[r:P:32, :].rearrange("p (g n) -> p g n", g=G), in_=rows[r])
+
+        load_scales(w4s_i, w4_scales)
+        load_w4(0)
+        load_r8(0)
+        load_scales(r8s_i, r8_scales)
+        for q in range(4):
+            nc.gpsimd.dma_start(
+                out=b_rows[32 * q : 32 * q + 8, :],
+                in_=b.rearrange("(m q j) -> q m j", q=4, j=32)[q],
+            )
+        nc.scalar.activation(out=warm_out[:], in_=warm[:], func=ACT.Silu)
+        for g in range(1, G):
+            load_x(g, 0, 0, TW)
+            load_w4(g)
+            load_r8(g)
+        for t in range(1, NT):
+            for g in range(G):
+                load_x(g, t, 0, TW)
+
+        def cast(g, t, c0, width, v_cols):
+            grouped = stage.tile([P, HALF, PACK], BF16, name="grouped", align_bytes=64)
+            nc.vector.tensor_copy(
+                out=grouped[:, :v_cols, :], in_=raw[g, t][:, :, c0 : c0 + v_cols].rearrange("p j w -> p w j")
+            )
+            if v_cols < width:
+                nc.scalar.copy(
+                    out=grouped[:, v_cols:width, :],
+                    in_=raw[g, t][:, :, c0 + v_cols : c0 + width].rearrange("p j w -> p w j"),
+                )
+            return grouped
+
+        def quantise(g, t, c0, width, grouped):
+            cols = slice(c0, c0 + width)
+            nc.vector.quantize_mx(
+                out=codes[g, t][:, cols].bitcast(FP8X4),
+                scales=planes[g, t][:, cols],
+                in_=grouped[:, :width, :].rearrange("p w j -> p (w j)"),
+            )
+
+        acc = {}
+
+        def mm_w4(m, g, t, c0=0, width=TW):
+            if g == 0:
+                acc[m] = psum.tile([P, TW], F32, name="bank%d" % ((m + c0 // P) % MT))
+            nc.tensor.matmul_mx(
+                out=acc[m][:, :width],
+                lhsT=w4[g][:, 256 * m : 256 * (m + 1)].bitcast(FP4X4),
+                lhsT_scale=w4s[:, g, P * m : P * (m + 1)],
+                rhs=codes[g, t][:, c0 : c0 + width].bitcast(FP8X4),
+                rhs_scale=planes[g, t][:, c0 : c0 + width],
+                start=(g == 0),
+                stop=False,
+            )
+
+        def mm_r8(m, g, t, c0=0, width=TW):
+            nc.tensor.matmul_mx(
+                out=acc[m][:, :width],
+                lhsT=r8[g][:, 512 * m : 512 * (m + 1)].bitcast(FP8X4),
+                lhsT_scale=r8s[:, g, P * m : P * (m + 1)],
+                rhs=codes[g, t][:, c0 : c0 + width].bitcast(FP8X4),
+                rhs_scale=planes[g, t][:, c0 : c0 + width],
+                start=False,
+                stop=(g == G - 1),
+            )
+
+        def finish(m, t):
+            res = outs.tile([P, TW], F32, name="res")
+            width = HALF if (t == NT - 1 and m == MT - 1) else TW
+            for c0 in range(0, TW, width):
+                cols = slice(c0, c0 + width)
+                nc.scalar.activation(out=res[:, cols], in_=acc[m][:, cols], func=ACT.Silu, bias=b_cols[:, m : m + 1])
+                nc.sync.dma_start(
+                    out=out[P * m : P * (m + 1), TW * t + c0 : TW * t + c0 + width], in_=res[:, cols]
+                )
+
+        def chunk(g, t, width, v_cols):
+            parts = [(c0, cast(g, t, c0, width, v_cols)) for c0 in range(0, TW, width)]
+            for c0, grouped in parts:
+                quantise(g, t, c0, width, grouped)
+
+        halves0 = cast(0, 0, 0, HALF, V_COLS)
+        quantise(0, 0, 0, HALF, halves0)
+        halves1 = cast(0, 0, 256, 128, 80)
+        halves2 = cast(0, 0, 384, 128, 80)
+        quantise(0, 0, 256, 128, halves1)
+        quantise(0, 0, 384, 128, halves2)
+        for m in range(MT):
+            mm_w4(m, 0, 0)
+        for m in range(MT):
+            mm_r8(m, 0, 0)
+
+        for g in range(1, G):
+            chunk(g, 0, HALF, V_COLS)
+        chunk(0, 1, HALF, HALF)
+        nc.vector.transpose(out=b_cols[:], in_=b_rows[:])
+        for g in range(1, G):
+            for m in range(MT):
+                mm_w4(m, g, 0)
+                mm_r8(m, g, 0)
+                if g == G - 1:
+                    finish(m, 0)
+        for g in range(1, G):
+            chunk(g, 1, HALF, HALF)
+        for g in range(G):
+            chunk(g, 2, HALF, HALF)
+        for g in range(G):
+            for m in range(MT):
+                mm_w4(m, g, 1)
+                mm_r8(m, g, 1)
+                if g == G - 1:
+                    finish(m, 1)
+        for m in range(MT):
+            for g in range(G):
+                mm_w4(m, g, 2)
+                mm_r8(m, g, 2)
+            finish(m, 2)

@@ -13,6 +13,7 @@ U8 = mybir.dt.uint8
 FP8X4 = mybir.dt.float8_e4m3fn_x4
 FP4X4 = mybir.dt.float4_e2m1fn_x4
 ACT = mybir.ActivationFunctionType
+ALU = mybir.AluOpType
 
 P = 128
 PACK = 4
@@ -21,46 +22,54 @@ MT = M // 128
 TW = 512
 NT = T // TW
 HALF = 256
-V_COLS = 160
+QUARTER = 128
+R8_ROW = 4
 
 
 def tile_mix_resid_fm_silu_kernel(tc, x, w4_words, w4_scales, r8_words, r8_scales, b, out):
     nc = tc.nc
     with ExitStack() as ctx:
         keep = ctx.enter_context(tc.tile_pool(name="keep", bufs=1))
-        stage = ctx.enter_context(tc.tile_pool(name="stage", bufs=6))
+        stage = ctx.enter_context(tc.tile_pool(name="stage", bufs=3))
         outs = ctx.enter_context(tc.tile_pool(name="outs", bufs=26))
         psum = ctx.enter_context(tc.psum_pool(name="psum", bufs=1))
         ctx.enter_context(tc.manual_schedule())
 
+        halved = [(0, 0), (0, 1), (1, 0)]
         raw = {}
         codes = {}
         planes = {}
         for t in range(NT):
             for g in range(G):
-                raw[g, t] = keep.tile([P, PACK, TW], F32, name="raw_%d_%d" % (g, t), align_bytes=64)
+                width = HALF if (g, t) in halved else TW
+                for c0 in range(0, TW, width):
+                    raw[g, t, c0] = keep.tile([P, PACK, width], F32, name="raw_%d_%d_%d" % (g, t, c0), align_bytes=64)
                 codes[g, t] = keep.tile([P, TW], U32, name="codes_%d_%d" % (g, t), align_bytes=256)
                 planes[g, t] = keep.tile([P, TW], U8, name="plane_%d_%d" % (g, t), align_bytes=256)
         w4 = [keep.tile([P, 2 * M], U8, name="w4_%d" % g, align_bytes=256) for g in range(G)]
         r8 = [keep.tile([P, 4 * M], U8, name="r8_%d" % g, align_bytes=256) for g in range(G)]
-        w4s = keep.tile([P, G, M], U8, name="w4s", align_bytes=256)
-        r8s = keep.tile([P, G, M], U8, name="r8s", align_bytes=256)
+        w4s_first = keep.tile([P, M], U8, name="w4s_first", align_bytes=256)
+        r8s_first = keep.tile([P, M], U8, name="r8s_first", align_bytes=256)
+        w4s_rest = keep.tile([P, (G - 1) * M], U8, name="w4s_rest", align_bytes=256)
+        r8s_rest = keep.tile([P, (G - 1) * M], U8, name="r8s_rest", align_bytes=256)
+        partial = [keep.tile([P, TW], F32, name="partial_%d" % m, align_bytes=64) for m in range(MT)]
         b_rows = keep.tile([P, 32], F32, name="b_rows", align_bytes=64)
         b_cols = keep.tile([P, 32], F32, name="b_cols", align_bytes=64)
         warm = keep.tile([P, 1], F32, name="warm")
         warm_out = keep.tile([P, 1], F32, name="warm_out")
 
-        w4s_i = w4s[:].rearrange("p g n -> p (g n)").bitcast(I32)
-        r8s_i = r8s[:].rearrange("p g n -> p (g n)").bitcast(I32)
-        nc.vector.memset(w4s_i, 0)
+        nc.vector.memset(w4s_first[:].bitcast(I32), 0)
         nc.vector.memset(warm[:], 0.0)
-        nc.gpsimd.memset(b_rows[:], 0.0)
-        nc.vector.memset(r8s_i, 0)
+        nc.vector.memset(b_rows[:], 0.0)
+        nc.vector.memset(r8s_first[:].bitcast(I32), 0)
+        nc.vector.memset(w4s_rest[:].bitcast(I32), 0)
+        nc.vector.memset(r8s_rest[:].bitcast(I32), 0)
 
-        def load_x(g, t, c0, c1):
+        def load_x(g, t, c0=0):
+            width = raw[g, t, c0].shape[2]
             nc.sync.dma_start(
-                out=raw[g, t][:, :, c0:c1],
-                in_=x[512 * g : 512 * (g + 1), TW * t + c0 : TW * t + c1].rearrange("(p j) t -> p j t", j=PACK),
+                out=raw[g, t, c0][:],
+                in_=x[512 * g : 512 * (g + 1), TW * t + c0 : TW * t + c0 + width].rearrange("(p j) t -> p j t", j=PACK),
             )
 
         def load_w4(g):
@@ -69,125 +78,156 @@ def tile_mix_resid_fm_silu_kernel(tc, x, w4_words, w4_scales, r8_words, r8_scale
         def load_r8(g):
             nc.sync.dma_start(out=r8[g][:].bitcast(I32), in_=r8_words[g].rearrange("p n i -> p (n i)").bitcast(I32))
 
-        load_x(0, 0, 0, HALF)
-        load_x(0, 0, HALF, TW)
-        def load_scales(view, scales):
+        def load_scales(tile, scales, g0, g1, row0):
             rows = scales.bitcast(I32).rearrange("g (q r) n -> r q g n", r=4)
+            view = tile[:].bitcast(I32)
             for r in range(4):
-                nc.sync.dma_start(out=view[r:P:32, :].rearrange("p (g n) -> p g n", g=G), in_=rows[r])
+                nc.sync.dma_start(
+                    out=view[row0 + r : P : 32, :].rearrange("p (g n) -> p g n", g=g1 - g0), in_=rows[r][:, g0:g1, :]
+                )
 
-        load_scales(w4s_i, w4_scales)
+        load_x(0, 0, 0)
+        load_scales(w4s_first, w4_scales, 0, 1, 0)
         load_w4(0)
+        load_x(0, 0, HALF)
         load_r8(0)
-        load_scales(r8s_i, r8_scales)
+        load_scales(r8s_first, r8_scales, 0, 1, R8_ROW)
         for q in range(4):
             nc.gpsimd.dma_start(
                 out=b_rows[32 * q : 32 * q + 8, :],
                 in_=b.rearrange("(m q j) -> q m j", q=4, j=32)[q],
             )
         nc.scalar.activation(out=warm_out[:], in_=warm[:], func=ACT.Silu)
-        for g in range(1, G):
-            load_x(g, 0, 0, TW)
-            load_w4(g)
-            load_r8(g)
-        for t in range(1, NT):
-            for g in range(G):
-                load_x(g, t, 0, TW)
+        load_x(0, 1, 0)
+        load_x(0, 1, HALF)
+        load_scales(w4s_rest, w4_scales, 1, G, 0)
+        load_x(1, 1)
+        load_w4(1)
+        load_r8(1)
+        load_scales(r8s_rest, r8_scales, 1, G, R8_ROW)
+        load_x(2, 1)
+        load_w4(2)
+        load_r8(2)
+        load_x(1, 0, 0)
+        load_x(1, 0, HALF)
+        load_x(2, 0)
+        for g in range(G):
+            load_x(g, 2)
 
-        def cast(g, t, c0, width, v_cols):
-            grouped = stage.tile([P, HALF, PACK], BF16, name="grouped", align_bytes=64)
-            nc.vector.tensor_copy(
-                out=grouped[:, :v_cols, :], in_=raw[g, t][:, :, c0 : c0 + v_cols].rearrange("p j w -> p w j")
-            )
+        def prepare(g, t, c0, v_cols):
+            source = raw[g, t, c0]
+            width = source.shape[2]
+            piece = width // 2
+            grouped = stage.tile([P, width, PACK], BF16, name="grouped", align_bytes=64)
+            for lo, hi in ((0, piece), (piece, v_cols)):
+                nc.vector.tensor_copy(out=grouped[:, lo:hi, :], in_=source[:, :, lo:hi].rearrange("p j w -> p w j"))
             if v_cols < width:
-                nc.scalar.copy(
-                    out=grouped[:, v_cols:width, :],
-                    in_=raw[g, t][:, :, c0 + v_cols : c0 + width].rearrange("p j w -> p w j"),
+                nc.scalar.copy(out=grouped[:, v_cols:, :], in_=source[:, :, v_cols:].rearrange("p j w -> p w j"))
+            for lo in (0, piece):
+                cols = slice(c0 + lo, c0 + lo + piece)
+                nc.vector.quantize_mx(
+                    out=codes[g, t][:, cols].bitcast(FP8X4),
+                    scales=planes[g, t][:, cols],
+                    in_=grouped[:, lo : lo + piece, :].rearrange("p w j -> p (w j)"),
                 )
-            return grouped
 
-        def quantise(g, t, c0, width, grouped):
-            cols = slice(c0, c0 + width)
-            nc.vector.quantize_mx(
-                out=codes[g, t][:, cols].bitcast(FP8X4),
-                scales=planes[g, t][:, cols],
-                in_=grouped[:, :width, :].rearrange("p w j -> p (w j)"),
-            )
+        def bank(i):
+            return psum.tile([P, TW], F32, name="bank%d" % i)
 
-        acc = {}
+        def mm_w4(acc, m, g, t, c0, width, start):
+            scale = w4s_first if g == 0 else w4s_rest
+            s0 = M * max(g - 1, 0) + P * m
+            step = TW if width == TW else QUARTER
+            for lo in range(c0, c0 + width, step):
+                nc.tensor.matmul_mx(
+                    out=acc[:, lo : lo + step],
+                    lhsT=w4[g][:, 256 * m : 256 * (m + 1)].bitcast(FP4X4),
+                    lhsT_scale=scale[:, s0 : s0 + P],
+                    rhs=codes[g, t][:, lo : lo + step].bitcast(FP8X4),
+                    rhs_scale=planes[g, t][:, lo : lo + step],
+                    start=(start and lo == c0),
+                    stop=False,
+                )
 
-        def mm_w4(m, g, t, c0=0, width=TW):
-            if g == 0:
-                acc[m] = psum.tile([P, TW], F32, name="bank%d" % ((m + c0 // P) % MT))
+        def mm_r8(acc, m, g, t, c0, width, stop):
+            scale = r8s_first if g == 0 else r8s_rest
+            s0 = M * max(g - 1, 0) + P * m
             nc.tensor.matmul_mx(
-                out=acc[m][:, :width],
-                lhsT=w4[g][:, 256 * m : 256 * (m + 1)].bitcast(FP4X4),
-                lhsT_scale=w4s[:, g, P * m : P * (m + 1)],
-                rhs=codes[g, t][:, c0 : c0 + width].bitcast(FP8X4),
-                rhs_scale=planes[g, t][:, c0 : c0 + width],
-                start=(g == 0),
-                stop=False,
-            )
-
-        def mm_r8(m, g, t, c0=0, width=TW):
-            nc.tensor.matmul_mx(
-                out=acc[m][:, :width],
+                out=acc[:, c0 : c0 + width],
                 lhsT=r8[g][:, 512 * m : 512 * (m + 1)].bitcast(FP8X4),
-                lhsT_scale=r8s[:, g, P * m : P * (m + 1)],
+                lhsT_scale=scale[R8_ROW:, s0 : s0 + P],
                 rhs=codes[g, t][:, c0 : c0 + width].bitcast(FP8X4),
                 rhs_scale=planes[g, t][:, c0 : c0 + width],
                 start=False,
-                stop=(g == G - 1),
+                stop=stop,
             )
 
-        def finish(m, t):
-            res = outs.tile([P, TW], F32, name="res")
-            width = HALF if (t == NT - 1 and m == MT - 1) else TW
-            for c0 in range(0, TW, width):
-                cols = slice(c0, c0 + width)
-                nc.scalar.activation(out=res[:, cols], in_=acc[m][:, cols], func=ACT.Silu, bias=b_cols[:, m : m + 1])
-                nc.sync.dma_start(
-                    out=out[P * m : P * (m + 1), TW * t + c0 : TW * t + c0 + width], in_=res[:, cols]
-                )
+        def finish(source, m, t, c0=0, width=TW):
+            res = outs.tile([P, width], F32, name="res")
+            nc.scalar.activation(out=res[:], in_=source[:, c0 : c0 + width], func=ACT.Silu, bias=b_cols[:, m : m + 1])
+            nc.sync.dma_start(out=out[P * m : P * (m + 1), TW * t + c0 : TW * t + c0 + width], in_=res[:])
 
-        def chunk(g, t, width, v_cols):
-            parts = [(c0, cast(g, t, c0, width, v_cols)) for c0 in range(0, TW, width)]
-            for c0, grouped in parts:
-                quantise(g, t, c0, width, grouped)
-
-        halves0 = cast(0, 0, 0, HALF, V_COLS)
-        quantise(0, 0, 0, HALF, halves0)
-        halves1 = cast(0, 0, 256, 128, 80)
-        halves2 = cast(0, 0, 384, 128, 80)
-        quantise(0, 0, 256, 128, halves1)
-        quantise(0, 0, 384, 128, halves2)
+        prepare(0, 0, 0, 176)
+        prepare(0, 0, HALF, 176)
+        acc = [bank(m) for m in range(MT)]
+        for c0 in (0, HALF):
+            for m in range(MT):
+                mm_w4(acc[m], m, 0, 0, c0, HALF, start=(c0 == 0))
         for m in range(MT):
-            mm_w4(m, 0, 0)
-        for m in range(MT):
-            mm_r8(m, 0, 0)
+            mm_r8(acc[m], m, 0, 0, 0, TW, stop=True)
+            nc.scalar.copy(out=partial[m][:], in_=acc[m][:])
 
-        for g in range(1, G):
-            chunk(g, 0, HALF, V_COLS)
-        chunk(0, 1, HALF, HALF)
+        prepare(0, 1, 0, HALF)
+        prepare(0, 1, HALF, HALF)
         nc.vector.transpose(out=b_cols[:], in_=b_rows[:])
-        for g in range(1, G):
-            for m in range(MT):
-                mm_w4(m, g, 0)
-                mm_r8(m, g, 0)
-                if g == G - 1:
-                    finish(m, 0)
-        for g in range(1, G):
-            chunk(g, 1, HALF, HALF)
-        for g in range(G):
-            chunk(g, 2, HALF, HALF)
-        for g in range(G):
-            for m in range(MT):
-                mm_w4(m, g, 1)
-                mm_r8(m, g, 1)
-                if g == G - 1:
-                    finish(m, 1)
+        prepare(1, 1, 0, 320)
+        acc = [bank(m) for m in range(MT)]
+        for c0 in (0, HALF):
+            for m in range(MT // 2):
+                mm_w4(acc[m], m, 0, 1, c0, HALF, start=(c0 == 0))
+                mm_r8(acc[m], m, 0, 1, c0, HALF, stop=False)
+        for m in range(MT // 2, MT):
+            mm_w4(acc[m], m, 0, 1, 0, TW, start=True)
+            mm_r8(acc[m], m, 0, 1, 0, TW, stop=False)
+        prepare(2, 1, 0, 320)
         for m in range(MT):
+            mm_w4(acc[m], m, 1, 1, 0, TW, start=False)
+        for m in range(MT):
+            mm_r8(acc[m], m, 1, 1, 0, TW, stop=False)
+        prepare(1, 0, 0, HALF)
+        prepare(1, 0, HALF, HALF)
+        for m in range(MT):
+            mm_w4(acc[m], m, 2, 1, 0, TW, start=False)
+            mm_r8(acc[m], m, 2, 1, 0, TW, stop=True)
+            finish(acc[m], m, 1)
+
+        prepare(2, 0, 0, 320)
+        prepare(0, 2, 0, 320)
+        acc = [bank(m) for m in range(MT)]
+        for m in range(MT):
+            mm_w4(acc[m], m, 1, 0, 0, TW, start=True)
+            mm_r8(acc[m], m, 1, 0, 0, TW, stop=False)
+        for m in range(MT):
+            mm_w4(acc[m], m, 2, 0, 0, TW, start=False)
+            mm_r8(acc[m], m, 2, 0, 0, TW, stop=True)
+            nc.vector.tensor_tensor(out=partial[m][:], in0=acc[m][:], in1=partial[m][:], op=ALU.add)
+            finish(partial[m], m, 0)
+
+        prepare(1, 2, 0, TW)
+        prepare(2, 2, 0, TW)
+        acc = [bank(m) for m in range(MT - 1)]
+        for m in range(MT - 1):
+            mm_w4(acc[m], m, 0, 2, 0, TW, start=True)
+            mm_r8(acc[m], m, 0, 2, 0, TW, stop=False)
+        for m in range(MT - 1):
+            for g in range(1, G):
+                mm_w4(acc[m], m, g, 2, 0, TW, start=False)
+                mm_r8(acc[m], m, g, 2, 0, TW, stop=(g == G - 1))
+            finish(acc[m], m, 2)
+        m = MT - 1
+        for i, (c0, width) in enumerate(((0, HALF), (HALF, QUARTER), (HALF + QUARTER, QUARTER))):
+            last = bank((m + i) % MT)
             for g in range(G):
-                mm_w4(m, g, 2)
-                mm_r8(m, g, 2)
-            finish(m, 2)
+                mm_w4(last, m, g, 2, c0, width, start=(g == 0))
+                mm_r8(last, m, g, 2, c0, width, stop=(g == G - 1))
+            finish(last, m, 2, c0, width)

@@ -31,7 +31,7 @@ def tile_mix_resid_fm_silu_kernel(tc, x, w4_words, w4_scales, r8_words, r8_scale
     with ExitStack() as ctx:
         keep = ctx.enter_context(tc.tile_pool(name="keep", bufs=1))
         stage = ctx.enter_context(tc.tile_pool(name="stage", bufs=3))
-        outs = ctx.enter_context(tc.tile_pool(name="outs", bufs=26))
+        outs = ctx.enter_context(tc.tile_pool(name="outs", bufs=10))
         psum = ctx.enter_context(tc.psum_pool(name="psum", bufs=1))
         ctx.enter_context(tc.manual_schedule())
 
@@ -53,6 +53,7 @@ def tile_mix_resid_fm_silu_kernel(tc, x, w4_words, w4_scales, r8_words, r8_scale
         w4s_rest = keep.tile([P, (G - 1) * M], U8, name="w4s_rest", align_bytes=256)
         r8s_rest = keep.tile([P, (G - 1) * M], U8, name="r8s_rest", align_bytes=256)
         partial = [keep.tile([P, TW], F32, name="partial_%d" % m, align_bytes=64) for m in range(MT)]
+        pair = [keep.tile([P, 2 * TW], F32, name="pair_%d" % m, align_bytes=64) for m in range(MT)]
         b_rows = keep.tile([P, 32], F32, name="b_rows", align_bytes=64)
         b_cols = keep.tile([P, 32], F32, name="b_cols", align_bytes=64)
         warm = keep.tile([P, 1], F32, name="warm")
@@ -60,10 +61,10 @@ def tile_mix_resid_fm_silu_kernel(tc, x, w4_words, w4_scales, r8_words, r8_scale
 
         nc.vector.memset(w4s_first[:].bitcast(I32), 0)
         nc.vector.memset(warm[:], 0.0)
-        nc.vector.memset(b_rows[:], 0.0)
         nc.vector.memset(r8s_first[:].bitcast(I32), 0)
         nc.vector.memset(w4s_rest[:].bitcast(I32), 0)
         nc.vector.memset(r8s_rest[:].bitcast(I32), 0)
+        nc.vector.memset(b_rows[:], 0.0)
 
         def load_x(g, t, c0=0):
             width = raw[g, t, c0].shape[2]
@@ -92,11 +93,6 @@ def tile_mix_resid_fm_silu_kernel(tc, x, w4_words, w4_scales, r8_words, r8_scale
         load_x(0, 0, HALF)
         load_r8(0)
         load_scales(r8s_first, r8_scales, 0, 1, R8_ROW)
-        for q in range(4):
-            nc.gpsimd.dma_start(
-                out=b_rows[32 * q : 32 * q + 8, :],
-                in_=b.rearrange("(m q j) -> q m j", q=4, j=32)[q],
-            )
         nc.scalar.activation(out=warm_out[:], in_=warm[:], func=ACT.Silu)
         load_x(0, 1, 0)
         load_x(0, 1, HALF)
@@ -106,6 +102,11 @@ def tile_mix_resid_fm_silu_kernel(tc, x, w4_words, w4_scales, r8_words, r8_scale
         load_r8(1)
         load_scales(r8s_rest, r8_scales, 1, G, R8_ROW)
         load_x(2, 1)
+        for q in range(4):
+            nc.sync.dma_start(
+                out=b_rows[32 * q : 32 * q + 8, :],
+                in_=b.rearrange("(m q j) -> q m j", q=4, j=32)[q],
+            )
         load_w4(2)
         load_r8(2)
         load_x(1, 0, 0)
@@ -149,7 +150,7 @@ def tile_mix_resid_fm_silu_kernel(tc, x, w4_words, w4_scales, r8_words, r8_scale
                     stop=False,
                 )
 
-        def mm_r8(acc, m, g, t, c0, width, stop):
+        def mm_r8(acc, m, g, t, c0, width, stop, start=False):
             scale = r8s_first if g == 0 else r8s_rest
             s0 = M * max(g - 1, 0) + P * m
             nc.tensor.matmul_mx(
@@ -158,7 +159,7 @@ def tile_mix_resid_fm_silu_kernel(tc, x, w4_words, w4_scales, r8_words, r8_scale
                 lhsT_scale=scale[R8_ROW:, s0 : s0 + P],
                 rhs=codes[g, t][:, c0 : c0 + width].bitcast(FP8X4),
                 rhs_scale=planes[g, t][:, c0 : c0 + width],
-                start=False,
+                start=start,
                 stop=stop,
             )
 
@@ -166,6 +167,11 @@ def tile_mix_resid_fm_silu_kernel(tc, x, w4_words, w4_scales, r8_words, r8_scale
             res = outs.tile([P, width], F32, name="res")
             nc.scalar.activation(out=res[:], in_=source[:, c0 : c0 + width], func=ACT.Silu, bias=b_cols[:, m : m + 1])
             nc.sync.dma_start(out=out[P * m : P * (m + 1), TW * t + c0 : TW * t + c0 + width], in_=res[:])
+
+        def silu_into_pair(source, m, t):
+            nc.scalar.activation(
+                out=pair[m][:, TW * t : TW * (t + 1)], in_=source[:], func=ACT.Silu, bias=b_cols[:, m : m + 1]
+            )
 
         prepare(0, 0, 0, 176)
         prepare(0, 0, HALF, 176)
@@ -179,7 +185,6 @@ def tile_mix_resid_fm_silu_kernel(tc, x, w4_words, w4_scales, r8_words, r8_scale
 
         prepare(0, 1, 0, HALF)
         prepare(0, 1, HALF, HALF)
-        nc.vector.transpose(out=b_cols[:], in_=b_rows[:])
         prepare(1, 1, 0, 320)
         acc = [bank(m) for m in range(MT)]
         for c0 in (0, HALF):
@@ -190,31 +195,41 @@ def tile_mix_resid_fm_silu_kernel(tc, x, w4_words, w4_scales, r8_words, r8_scale
             mm_w4(acc[m], m, 0, 1, 0, TW, start=True)
             mm_r8(acc[m], m, 0, 1, 0, TW, stop=False)
         prepare(2, 1, 0, 320)
+        nc.vector.transpose(out=b_cols[:], in_=b_rows[:])
         for m in range(MT):
             mm_w4(acc[m], m, 1, 1, 0, TW, start=False)
         for m in range(MT):
             mm_r8(acc[m], m, 1, 1, 0, TW, stop=False)
         prepare(1, 0, 0, HALF)
         prepare(1, 0, HALF, HALF)
-        for m in range(MT):
+        for m in range(MT // 2):
             mm_w4(acc[m], m, 2, 1, 0, TW, start=False)
+        for m in range(MT):
             mm_r8(acc[m], m, 2, 1, 0, TW, stop=True)
-            finish(acc[m], m, 1)
+            silu_into_pair(acc[m], m, 1)
+            if m < MT // 2:
+                mm_w4(acc[m + MT // 2], m + MT // 2, 2, 1, 0, TW, start=False)
 
         prepare(2, 0, 0, 320)
         prepare(0, 2, 0, 320)
         acc = [bank(m) for m in range(MT)]
-        for m in range(MT):
+        for m in range(MT // 2):
+            mm_r8(acc[m], m, 1, 0, 0, HALF, stop=False, start=True)
+        for m in range(MT // 2):
+            mm_r8(acc[m], m, 1, 0, HALF, HALF, stop=False)
+            mm_w4(acc[m], m, 1, 0, 0, TW, start=False)
+        for m in range(MT // 2, MT):
             mm_w4(acc[m], m, 1, 0, 0, TW, start=True)
             mm_r8(acc[m], m, 1, 0, 0, TW, stop=False)
         for m in range(MT):
             mm_w4(acc[m], m, 2, 0, 0, TW, start=False)
             mm_r8(acc[m], m, 2, 0, 0, TW, stop=True)
             nc.vector.tensor_tensor(out=partial[m][:], in0=acc[m][:], in1=partial[m][:], op=ALU.add)
-            finish(partial[m], m, 0)
+            silu_into_pair(partial[m], m, 0)
+            nc.sync.dma_start(out=out[P * m : P * (m + 1), : 2 * TW], in_=pair[m][:])
 
-        prepare(1, 2, 0, TW)
-        prepare(2, 2, 0, TW)
+        prepare(1, 2, 0, 384)
+        prepare(2, 2, 0, 320)
         acc = [bank(m) for m in range(MT - 1)]
         for m in range(MT - 1):
             mm_w4(acc[m], m, 0, 2, 0, TW, start=True)

@@ -60,10 +60,10 @@ def tile_mix_resid_fm_silu_kernel(tc, x, w4_words, w4_scales, r8_words, r8_scale
         warm_out = keep.tile([P, 1], F32, name="warm_out")
 
         nc.vector.memset(w4s_first[:].bitcast(I32), 0)
+        nc.vector.memset(r8s_rest[:].bitcast(I32), 0)
         nc.vector.memset(warm[:], 0.0)
         nc.vector.memset(r8s_first[:].bitcast(I32), 0)
         nc.vector.memset(w4s_rest[:].bitcast(I32), 0)
-        nc.vector.memset(r8s_rest[:].bitcast(I32), 0)
         nc.vector.memset(b_rows[:], 0.0)
 
         def load_x(g, t, c0=0):
@@ -76,31 +76,33 @@ def tile_mix_resid_fm_silu_kernel(tc, x, w4_words, w4_scales, r8_words, r8_scale
         def load_w4(g):
             nc.sync.dma_start(out=w4[g][:].bitcast(I32), in_=w4_words[g].bitcast(I32))
 
-        def load_r8(g):
-            nc.sync.dma_start(out=r8[g][:].bitcast(I32), in_=r8_words[g].rearrange("p n i -> p (n i)").bitcast(I32))
+        def load_r8(g, n0=0, n1=M):
+            words = r8_words[g].rearrange("p n i -> p (n i)").bitcast(I32)
+            nc.sync.dma_start(out=r8[g][:].bitcast(I32)[:, n0:n1], in_=words[:, n0:n1])
 
-        def load_scales(tile, scales, g0, g1, row0):
+        def load_scales(queue, tile, scales, g0, g1, row0):
             rows = scales.bitcast(I32).rearrange("g (q r) n -> r q g n", r=4)
             view = tile[:].bitcast(I32)
             for r in range(4):
-                nc.sync.dma_start(
+                queue.dma_start(
                     out=view[row0 + r : P : 32, :].rearrange("p (g n) -> p g n", g=g1 - g0), in_=rows[r][:, g0:g1, :]
                 )
 
         load_x(0, 0, 0)
-        load_scales(w4s_first, w4_scales, 0, 1, 0)
+        load_scales(nc.sync, w4s_first, w4_scales, 0, 1, 0)
+        load_scales(nc.gpsimd, r8s_rest, r8_scales, 1, G, R8_ROW)
         load_w4(0)
         load_x(0, 0, HALF)
-        load_r8(0)
-        load_scales(r8s_first, r8_scales, 0, 1, R8_ROW)
+        load_r8(0, 0, M // 2)
+        load_scales(nc.sync, r8s_first, r8_scales, 0, 1, R8_ROW)
+        load_r8(0, M // 2, M)
         nc.scalar.activation(out=warm_out[:], in_=warm[:], func=ACT.Silu)
         load_x(0, 1, 0)
         load_x(0, 1, HALF)
-        load_scales(w4s_rest, w4_scales, 1, G, 0)
+        load_scales(nc.sync, w4s_rest, w4_scales, 1, G, 0)
         load_x(1, 1)
         load_w4(1)
         load_r8(1)
-        load_scales(r8s_rest, r8_scales, 1, G, R8_ROW)
         load_x(2, 1)
         for q in range(4):
             nc.sync.dma_start(
@@ -176,9 +178,9 @@ def tile_mix_resid_fm_silu_kernel(tc, x, w4_words, w4_scales, r8_words, r8_scale
         prepare(0, 0, 0, 176)
         prepare(0, 0, HALF, 176)
         acc = [bank(m) for m in range(MT)]
-        for c0 in (0, HALF):
+        for c0 in range(0, TW, QUARTER):
             for m in range(MT):
-                mm_w4(acc[m], m, 0, 0, c0, HALF, start=(c0 == 0))
+                mm_w4(acc[m], m, 0, 0, c0, QUARTER, start=(c0 == 0))
         for m in range(MT):
             mm_r8(acc[m], m, 0, 0, 0, TW, stop=True)
             nc.scalar.copy(out=partial[m][:], in_=acc[m][:])

@@ -24,6 +24,10 @@ NT = T // TW
 HALF = 256
 QUARTER = 128
 R8_ROW = 4
+HEAD_SPLIT = 176
+SPLIT = 320
+LEAD = 2
+PARKED = [(0, m) for m in range(MT)]
 
 
 def tile_mix_resid_fm_silu_kernel(tc, x, w4_words, w4_scales, r8_words, r8_scales, b, out):
@@ -35,15 +39,11 @@ def tile_mix_resid_fm_silu_kernel(tc, x, w4_words, w4_scales, r8_words, r8_scale
         psum = ctx.enter_context(tc.psum_pool(name="psum", bufs=1))
         ctx.enter_context(tc.manual_schedule())
 
-        halved = [(0, 0), (0, 1), (1, 0)]
         raw = {}
         codes = {}
         planes = {}
         for t in range(NT):
             for g in range(G):
-                width = HALF if (g, t) in halved else TW
-                for c0 in range(0, TW, width):
-                    raw[g, t, c0] = keep.tile([P, PACK, width], F32, name="raw_%d_%d_%d" % (g, t, c0), align_bytes=64)
                 codes[g, t] = keep.tile([P, TW], U32, name="codes_%d_%d" % (g, t), align_bytes=256)
                 planes[g, t] = keep.tile([P, TW], U8, name="plane_%d_%d" % (g, t), align_bytes=256)
         w4 = [keep.tile([P, 2 * M], U8, name="w4_%d" % g, align_bytes=256) for g in range(G)]
@@ -52,26 +52,27 @@ def tile_mix_resid_fm_silu_kernel(tc, x, w4_words, w4_scales, r8_words, r8_scale
         r8s_first = keep.tile([P, M], U8, name="r8s_first", align_bytes=256)
         w4s_rest = keep.tile([P, (G - 1) * M], U8, name="w4s_rest", align_bytes=256)
         r8s_rest = keep.tile([P, (G - 1) * M], U8, name="r8s_rest", align_bytes=256)
-        partial = [keep.tile([P, TW], F32, name="partial_%d" % m, align_bytes=64) for m in range(MT)]
+        parked = {
+            (t, m): keep.tile([P, TW], F32, name="parked_%d_%d" % (t, m), align_bytes=64)
+            for t, m in PARKED
+        }
         pair = [keep.tile([P, 2 * TW], F32, name="pair_%d" % m, align_bytes=64) for m in range(MT)]
         b_rows = keep.tile([P, 32], F32, name="b_rows", align_bytes=64)
         b_cols = keep.tile([P, 32], F32, name="b_cols", align_bytes=64)
-        warm = keep.tile([P, 1], F32, name="warm")
-        warm_out = keep.tile([P, 1], F32, name="warm_out")
 
         nc.vector.memset(w4s_first[:].bitcast(I32), 0)
-        nc.vector.memset(r8s_rest[:].bitcast(I32), 0)
-        nc.vector.memset(warm[:], 0.0)
-        nc.vector.memset(r8s_first[:].bitcast(I32), 0)
         nc.vector.memset(w4s_rest[:].bitcast(I32), 0)
+        nc.vector.memset(r8s_first[:].bitcast(I32), 0)
+        nc.vector.memset(r8s_rest[:].bitcast(I32), 0)
         nc.vector.memset(b_rows[:], 0.0)
 
-        def load_x(g, t, c0=0):
-            width = raw[g, t, c0].shape[2]
+        def load_x(g, c0, width):
+            tile = keep.tile([P, PACK, width], F32, name="raw_%d_%d" % (g, c0), align_bytes=64)
             nc.sync.dma_start(
-                out=raw[g, t, c0][:],
-                in_=x[512 * g : 512 * (g + 1), TW * t + c0 : TW * t + c0 + width].rearrange("(p j) t -> p j t", j=PACK),
+                out=tile[:], in_=x[512 * g : 512 * (g + 1), c0 : c0 + width].rearrange("(p j) t -> p j t", j=PACK)
             )
+            for lo in range(0, width, QUARTER):
+                raw[g, c0 + lo] = (tile, lo)
 
         def load_w4(g):
             nc.sync.dma_start(out=w4[g][:].bitcast(I32), in_=w4_words[g].bitcast(I32))
@@ -88,44 +89,44 @@ def tile_mix_resid_fm_silu_kernel(tc, x, w4_words, w4_scales, r8_words, r8_scale
                     out=view[row0 + r : P : 32, :].rearrange("p (g n) -> p g n", g=g1 - g0), in_=rows[r][:, g0:g1, :]
                 )
 
-        load_x(0, 0, 0)
-        load_scales(nc.sync, w4s_first, w4_scales, 0, 1, 0)
-        load_scales(nc.gpsimd, r8s_rest, r8_scales, 1, G, R8_ROW)
-        load_w4(0)
+        def load_bias(queue):
+            queue.dma_start(out=b_rows[0:P:4, :], in_=b.rearrange("(m q j) -> q m j", q=4, j=32))
+
         load_x(0, 0, HALF)
+        load_scales(nc.sync, w4s_first, w4_scales, 0, 1, 0)
+        load_scales(nc.gpsimd, w4s_rest, w4_scales, 1, G, 0)
+        load_scales(nc.gpsimd, r8s_rest, r8_scales, 1, G, R8_ROW)
+        load_bias(nc.gpsimd)
+        load_w4(0)
+        load_x(0, HALF, HALF)
         load_r8(0, 0, M // 2)
         load_scales(nc.sync, r8s_first, r8_scales, 0, 1, R8_ROW)
         load_r8(0, M // 2, M)
-        nc.scalar.activation(out=warm_out[:], in_=warm[:], func=ACT.Silu)
-        load_x(0, 1, 0)
-        load_x(0, 1, HALF)
-        load_scales(nc.sync, w4s_rest, w4_scales, 1, G, 0)
-        load_x(1, 1)
-        load_w4(1)
-        load_r8(1)
-        load_x(2, 1)
-        for q in range(4):
-            nc.sync.dma_start(
-                out=b_rows[32 * q : 32 * q + 8, :],
-                in_=b.rearrange("(m q j) -> q m j", q=4, j=32)[q],
-            )
-        load_w4(2)
-        load_r8(2)
-        load_x(1, 0, 0)
+        load_x(0, TW, HALF)
+        load_x(0, TW + HALF, HALF)
+        for g in range(1, G):
+            load_x(g, TW, TW)
+            load_w4(g)
+            load_r8(g)
         load_x(1, 0, HALF)
-        load_x(2, 0)
+        load_x(1, HALF, HALF)
+        load_x(2, 0, TW)
         for g in range(G):
-            load_x(g, 2)
+            load_x(g, 2 * TW, TW)
 
-        def prepare(g, t, c0, v_cols):
-            source = raw[g, t, c0]
-            width = source.shape[2]
-            piece = width // 2
+        def cast(g, t, c0=0, width=TW, v_cols=None):
+            tile, at = raw[g, TW * t + c0]
+            source = tile[:, :, at : at + width]
+            v_cols = v_cols or width
             grouped = stage.tile([P, width, PACK], BF16, name="grouped", align_bytes=64)
-            for lo, hi in ((0, piece), (piece, v_cols)):
+            for lo, hi in ((0, width // 2), (width // 2, v_cols)):
                 nc.vector.tensor_copy(out=grouped[:, lo:hi, :], in_=source[:, :, lo:hi].rearrange("p j w -> p w j"))
             if v_cols < width:
                 nc.scalar.copy(out=grouped[:, v_cols:, :], in_=source[:, :, v_cols:].rearrange("p j w -> p w j"))
+            return grouped
+
+        def quantise(grouped, g, t, c0=0):
+            piece = grouped.shape[1] // 2
             for lo in (0, piece):
                 cols = slice(c0 + lo, c0 + lo + piece)
                 nc.vector.quantize_mx(
@@ -134,10 +135,13 @@ def tile_mix_resid_fm_silu_kernel(tc, x, w4_words, w4_scales, r8_words, r8_scale
                     in_=grouped[:, lo : lo + piece, :].rearrange("p w j -> p (w j)"),
                 )
 
-        def bank(i):
-            return psum.tile([P, TW], F32, name="bank%d" % i)
+        def prepare(g, t, c0=0, width=TW, v_cols=None):
+            quantise(cast(g, t, c0, width, v_cols), g, t, c0)
 
-        def mm_w4(acc, m, g, t, c0, width, start):
+        def bank(i):
+            return psum.tile([P, TW], F32, name="bank%d" % (i % MT))
+
+        def mm_w4(acc, m, g, t, c0=0, width=TW, start=False, stop=False):
             scale = w4s_first if g == 0 else w4s_rest
             s0 = M * max(g - 1, 0) + P * m
             step = TW if width == TW else QUARTER
@@ -149,10 +153,10 @@ def tile_mix_resid_fm_silu_kernel(tc, x, w4_words, w4_scales, r8_words, r8_scale
                     rhs=codes[g, t][:, lo : lo + step].bitcast(FP8X4),
                     rhs_scale=planes[g, t][:, lo : lo + step],
                     start=(start and lo == c0),
-                    stop=False,
+                    stop=(stop and lo + step == c0 + width),
                 )
 
-        def mm_r8(acc, m, g, t, c0, width, stop, start=False):
+        def mm_r8(acc, m, g, t, c0=0, width=TW, start=False, stop=False):
             scale = r8s_first if g == 0 else r8s_rest
             s0 = M * max(g - 1, 0) + P * m
             nc.tensor.matmul_mx(
@@ -165,85 +169,97 @@ def tile_mix_resid_fm_silu_kernel(tc, x, w4_words, w4_scales, r8_words, r8_scale
                 stop=stop,
             )
 
+        def both(acc, m, g, t, start=False, stop=False):
+            mm_w4(acc, m, g, t, start=start)
+            mm_r8(acc, m, g, t, stop=stop)
+
+        def park(acc, m, t):
+            nc.scalar.copy(out=parked[t, m][:], in_=acc[:])
+
+        def silu(target, source, m):
+            nc.scalar.activation(out=target, in_=source, func=ACT.Silu, bias=b_cols[:, 4 * m : 4 * m + 1])
+
+        def add_parked(acc, m, t, c0=0, width=TW):
+            cols = slice(c0, c0 + width)
+            nc.vector.tensor_tensor(out=parked[t, m][:, cols], in0=acc[:, cols], in1=parked[t, m][:, cols], op=ALU.add)
+
+        def store(source, m, c0, width):
+            nc.sync.dma_start(out=out[P * m : P * (m + 1), c0 : c0 + width], in_=source)
+
         def finish(source, m, t, c0=0, width=TW):
             res = outs.tile([P, width], F32, name="res")
-            nc.scalar.activation(out=res[:], in_=source[:, c0 : c0 + width], func=ACT.Silu, bias=b_cols[:, m : m + 1])
-            nc.sync.dma_start(out=out[P * m : P * (m + 1), TW * t + c0 : TW * t + c0 + width], in_=res[:])
+            silu(res[:], source[:, c0 : c0 + width], m)
+            store(res[:], m, TW * t + c0, width)
 
-        def silu_into_pair(source, m, t):
-            nc.scalar.activation(
-                out=pair[m][:, TW * t : TW * (t + 1)], in_=source[:], func=ACT.Silu, bias=b_cols[:, m : m + 1]
-            )
-
-        prepare(0, 0, 0, 176)
-        prepare(0, 0, HALF, 176)
+        prepare(0, 0, 0, HALF, HEAD_SPLIT)
+        prepare(0, 0, HALF, HALF, HEAD_SPLIT)
         acc = [bank(m) for m in range(MT)]
         for c0 in range(0, TW, QUARTER):
             for m in range(MT):
                 mm_w4(acc[m], m, 0, 0, c0, QUARTER, start=(c0 == 0))
         for m in range(MT):
-            mm_r8(acc[m], m, 0, 0, 0, TW, stop=True)
-            nc.scalar.copy(out=partial[m][:], in_=acc[m][:])
+            mm_r8(acc[m], m, 0, 0, stop=True)
+            park(acc[m], m, 0)
 
         prepare(0, 1, 0, HALF)
         prepare(0, 1, HALF, HALF)
-        prepare(1, 1, 0, 320)
+        prepare(1, 1, 0, TW, SPLIT)
         acc = [bank(m) for m in range(MT)]
         for c0 in (0, HALF):
             for m in range(MT // 2):
                 mm_w4(acc[m], m, 0, 1, c0, HALF, start=(c0 == 0))
-                mm_r8(acc[m], m, 0, 1, c0, HALF, stop=False)
+                mm_r8(acc[m], m, 0, 1, c0, HALF)
         for m in range(MT // 2, MT):
-            mm_w4(acc[m], m, 0, 1, 0, TW, start=True)
-            mm_r8(acc[m], m, 0, 1, 0, TW, stop=False)
-        prepare(2, 1, 0, 320)
+            both(acc[m], m, 0, 1, start=True)
+        prepare(2, 1, 0, TW, SPLIT)
         nc.vector.transpose(out=b_cols[:], in_=b_rows[:])
         for m in range(MT):
-            mm_w4(acc[m], m, 1, 1, 0, TW, start=False)
+            mm_w4(acc[m], m, 1, 1)
         for m in range(MT):
-            mm_r8(acc[m], m, 1, 1, 0, TW, stop=False)
+            mm_r8(acc[m], m, 1, 1)
         prepare(1, 0, 0, HALF)
         prepare(1, 0, HALF, HALF)
         for m in range(MT // 2):
-            mm_w4(acc[m], m, 2, 1, 0, TW, start=False)
+            mm_w4(acc[m], m, 2, 1)
         for m in range(MT):
-            mm_r8(acc[m], m, 2, 1, 0, TW, stop=True)
-            silu_into_pair(acc[m], m, 1)
+            mm_r8(acc[m], m, 2, 1, stop=True)
+            silu(pair[m][:, TW:], acc[m][:], m)
             if m < MT // 2:
-                mm_w4(acc[m + MT // 2], m + MT // 2, 2, 1, 0, TW, start=False)
+                mm_w4(acc[m + MT // 2], m + MT // 2, 2, 1)
 
-        prepare(2, 0, 0, 320)
-        prepare(0, 2, 0, 320)
+        prepare(2, 0, 0, TW, SPLIT)
+        prepare(0, 2, 0, TW, SPLIT)
         acc = [bank(m) for m in range(MT)]
         for m in range(MT // 2):
-            mm_r8(acc[m], m, 1, 0, 0, HALF, stop=False, start=True)
+            mm_r8(acc[m], m, 1, 0, 0, HALF, start=True)
         for m in range(MT // 2):
-            mm_r8(acc[m], m, 1, 0, HALF, HALF, stop=False)
-            mm_w4(acc[m], m, 1, 0, 0, TW, start=False)
+            mm_r8(acc[m], m, 1, 0, HALF, HALF)
+            mm_w4(acc[m], m, 1, 0)
         for m in range(MT // 2, MT):
-            mm_w4(acc[m], m, 1, 0, 0, TW, start=True)
-            mm_r8(acc[m], m, 1, 0, 0, TW, stop=False)
+            both(acc[m], m, 1, 0, start=True)
         for m in range(MT):
-            mm_w4(acc[m], m, 2, 0, 0, TW, start=False)
-            mm_r8(acc[m], m, 2, 0, 0, TW, stop=True)
-            nc.vector.tensor_tensor(out=partial[m][:], in0=acc[m][:], in1=partial[m][:], op=ALU.add)
-            silu_into_pair(partial[m], m, 0)
-            nc.sync.dma_start(out=out[P * m : P * (m + 1), : 2 * TW], in_=pair[m][:])
+            both(acc[m], m, 2, 0, stop=True)
+            add_parked(acc[m], m, 0)
+            silu(pair[m][:, :TW], parked[0, m][:], m)
+            store(pair[m][:], m, 0, 2 * TW)
+            if m == 7:
+                prepare(1, 2, 0, TW, 384)
+            if m == 7:
+                prepare(2, 2, 0, TW, 320)
 
-        prepare(1, 2, 0, 384)
-        prepare(2, 2, 0, 320)
         acc = [bank(m) for m in range(MT - 1)]
         for m in range(MT - 1):
-            mm_w4(acc[m], m, 0, 2, 0, TW, start=True)
-            mm_r8(acc[m], m, 0, 2, 0, TW, stop=False)
-        for m in range(MT - 1):
-            for g in range(1, G):
-                mm_w4(acc[m], m, g, 2, 0, TW, start=False)
-                mm_r8(acc[m], m, g, 2, 0, TW, stop=(g == G - 1))
-            finish(acc[m], m, 2)
+            both(acc[m], m, 0, 2, start=True)
+        for step in range(MT - 1 + LEAD):
+            if step < MT - 1:
+                both(acc[step], step, 1, 2)
+            m = step - LEAD
+            if m >= 0:
+                both(acc[m], m, 2, 2, stop=True)
+                finish(acc[m], m, 2)
         m = MT - 1
         for i, (c0, width) in enumerate(((0, HALF), (HALF, QUARTER), (HALF + QUARTER, QUARTER))):
-            last = bank((m + i) % MT)
+            last = bank(m + i)
             for g in range(G):
                 mm_w4(last, m, g, 2, c0, width, start=(g == 0))
                 mm_r8(last, m, g, 2, c0, width, stop=(g == G - 1))

@@ -26,7 +26,9 @@ QUARTER = 128
 R8_ROW = 4
 HEAD_SPLIT = 176
 SPLIT = 320
-LEAD = 2
+LEAD = 3
+LEAD_PARKED = 2
+HELD = 2
 PARKED = [(0, m) for m in range(MT)]
 
 
@@ -35,7 +37,7 @@ def tile_mix_resid_fm_silu_kernel(tc, x, w4_words, w4_scales, r8_words, r8_scale
     with ExitStack() as ctx:
         keep = ctx.enter_context(tc.tile_pool(name="keep", bufs=1))
         stage = ctx.enter_context(tc.tile_pool(name="stage", bufs=3))
-        outs = ctx.enter_context(tc.tile_pool(name="outs", bufs=10))
+        outs = ctx.enter_context(tc.tile_pool(name="outs", bufs=12))
         psum = ctx.enter_context(tc.psum_pool(name="psum", bufs=1))
         ctx.enter_context(tc.manual_schedule())
 
@@ -108,11 +110,10 @@ def tile_mix_resid_fm_silu_kernel(tc, x, w4_words, w4_scales, r8_words, r8_scale
             load_x(g, TW, TW)
             load_w4(g)
             load_r8(g)
-        load_x(1, 0, HALF)
-        load_x(1, HALF, HALF)
-        load_x(2, 0, TW)
         for g in range(G):
             load_x(g, 2 * TW, TW)
+        for g in range(1, G):
+            load_x(g, 0, TW)
 
         def cast(g, t, c0=0, width=TW, v_cols=None):
             tile, at = raw[g, TW * t + c0]
@@ -194,22 +195,29 @@ def tile_mix_resid_fm_silu_kernel(tc, x, w4_words, w4_scales, r8_words, r8_scale
         prepare(0, 0, 0, HALF, HEAD_SPLIT)
         prepare(0, 0, HALF, HALF, HEAD_SPLIT)
         acc = [bank(m) for m in range(MT)]
-        for c0 in range(0, TW, QUARTER):
+        for c0 in (0, QUARTER):
             for m in range(MT):
                 mm_w4(acc[m], m, 0, 0, c0, QUARTER, start=(c0 == 0))
+        for c0 in (HALF, HALF + QUARTER):
+            for m in range(8):
+                mm_w4(acc[m], m, 0, 0, c0, QUARTER)
         for m in range(MT):
             mm_r8(acc[m], m, 0, 0, stop=True)
-            park(acc[m], m, 0)
+            if m < MT - 2:
+                park(acc[m], m, 0)
 
         prepare(0, 1, 0, HALF)
         prepare(0, 1, HALF, HALF)
+        for m in range(MT - 2, MT):
+            nc.vector.tensor_copy(out=parked[0, m][:], in_=acc[m][:])
         prepare(1, 1, 0, TW, SPLIT)
         acc = [bank(m) for m in range(MT)]
         for c0 in (0, HALF):
-            for m in range(MT // 2):
-                mm_w4(acc[m], m, 0, 1, c0, HALF, start=(c0 == 0))
-                mm_r8(acc[m], m, 0, 1, c0, HALF)
-        for m in range(MT // 2, MT):
+            for m in range(4):
+                if m < 4:
+                    mm_w4(acc[m], m, 0, 1, c0, HALF, start=(c0 == 0))
+                mm_r8(acc[m], m, 0, 1, c0, HALF, start=(c0 == 0 and m >= 4))
+        for m in range(4, MT):
             both(acc[m], m, 0, 1, start=True)
         prepare(2, 1, 0, TW, SPLIT)
         nc.vector.transpose(out=b_cols[:], in_=b_rows[:])
@@ -217,46 +225,54 @@ def tile_mix_resid_fm_silu_kernel(tc, x, w4_words, w4_scales, r8_words, r8_scale
             mm_w4(acc[m], m, 1, 1)
         for m in range(MT):
             mm_r8(acc[m], m, 1, 1)
-        prepare(1, 0, 0, HALF)
-        prepare(1, 0, HALF, HALF)
+        prepare(0, 2, 0, HALF)
+        prepare(0, 2, HALF, HALF)
         for m in range(MT // 2):
             mm_w4(acc[m], m, 2, 1)
         for m in range(MT):
             mm_r8(acc[m], m, 2, 1, stop=True)
-            silu(pair[m][:, TW:], acc[m][:], m)
+            silu(pair[m][:, :TW], acc[m][:], m)
             if m < MT // 2:
                 mm_w4(acc[m + MT // 2], m + MT // 2, 2, 1)
 
-        prepare(2, 0, 0, TW, SPLIT)
-        prepare(0, 2, 0, TW, SPLIT)
-        acc = [bank(m) for m in range(MT)]
-        for m in range(MT // 2):
-            mm_r8(acc[m], m, 1, 0, 0, HALF, start=True)
-        for m in range(MT // 2):
-            mm_r8(acc[m], m, 1, 0, HALF, HALF)
-            mm_w4(acc[m], m, 1, 0)
-        for m in range(MT // 2, MT):
-            both(acc[m], m, 1, 0, start=True)
-        for m in range(MT):
-            both(acc[m], m, 2, 0, stop=True)
-            add_parked(acc[m], m, 0)
-            silu(pair[m][:, :TW], parked[0, m][:], m)
-            store(pair[m][:], m, 0, 2 * TW)
-            if m == 7:
-                prepare(1, 2, 0, TW, 384)
-            if m == 7:
-                prepare(2, 2, 0, TW, 320)
-
-        acc = [bank(m) for m in range(MT - 1)]
-        for m in range(MT - 1):
+        prepare(1, 2, 0, TW, 512)
+        prepare(2, 2, 0, TW, 320)
+        acc = [bank(m) for m in range(MT - HELD)]
+        for c0 in (0, HALF):
+            for m in range(4):
+                mm_r8(acc[m], m, 0, 2, c0, HALF, start=(c0 == 0))
+        for m in range(4):
+            mm_w4(acc[m], m, 0, 2)
+        for m in range(4, MT - HELD):
             both(acc[m], m, 0, 2, start=True)
-        for step in range(MT - 1 + LEAD):
-            if step < MT - 1:
+        for m in range(MT - HELD, MT):
+            store(pair[m][:, :TW], m, TW, TW)
+        prepare(1, 0)
+        prepare(2, 0)
+        for step in range(MT - HELD + LEAD):
+            if step < MT - HELD:
                 both(acc[step], step, 1, 2)
             m = step - LEAD
             if m >= 0:
                 both(acc[m], m, 2, 2, stop=True)
-                finish(acc[m], m, 2)
+                silu(pair[m][:, TW:], acc[m][:], m)
+                store(pair[m][:], m, TW, 2 * TW)
+
+        acc = {}
+        for step in range(MT + LEAD_PARKED):
+            if step < MT:
+                acc[step] = bank(step + MT - HELD)
+                both(acc[step], step, 1, 0, start=True)
+            m = step - LEAD_PARKED
+            if m >= 0:
+                both(acc[m], m, 2, 0, stop=True)
+                add_parked(acc[m], m, 0)
+                finish(parked[0, m], m, 0)
+        for m in range(MT - HELD, MT - 1):
+            one = bank(m)
+            for g in range(G):
+                both(one, m, g, 2, start=(g == 0), stop=(g == G - 1))
+            finish(one, m, 2)
         m = MT - 1
         for i, (c0, width) in enumerate(((0, HALF), (HALF, QUARTER), (HALF + QUARTER, QUARTER))):
             last = bank(m + i)

@@ -63,10 +63,8 @@ def tile_mix_resid_fm_silu_kernel(tc, x, w4_words, w4_scales, r8_words, r8_scale
         b_cols = keep.tile([P, 32], F32, name="b_cols", align_bytes=64)
 
         nc.vector.memset(w4s_first[:].bitcast(I32), 0)
-        nc.vector.memset(w4s_rest[:].bitcast(I32), 0)
         nc.vector.memset(r8s_first[:].bitcast(I32), 0)
-        nc.vector.memset(r8s_rest[:].bitcast(I32), 0)
-        nc.vector.memset(b_rows[:], 0.0)
+        nc.vector.memset(w4s_rest[:].bitcast(I32), 0)
 
         def load_x(g, c0, width):
             tile = keep.tile([P, PACK, width], F32, name="raw_%d_%d" % (g, c0), align_bytes=64)
@@ -97,8 +95,6 @@ def tile_mix_resid_fm_silu_kernel(tc, x, w4_words, w4_scales, r8_words, r8_scale
         load_x(0, 0, HALF)
         load_scales(nc.sync, w4s_first, w4_scales, 0, 1, 0)
         load_scales(nc.gpsimd, w4s_rest, w4_scales, 1, G, 0)
-        load_scales(nc.gpsimd, r8s_rest, r8_scales, 1, G, R8_ROW)
-        load_bias(nc.gpsimd)
         load_w4(0)
         load_x(0, HALF, HALF)
         load_r8(0, 0, M // 2)
@@ -194,6 +190,10 @@ def tile_mix_resid_fm_silu_kernel(tc, x, w4_words, w4_scales, r8_words, r8_scale
 
         prepare(0, 0, 0, HALF, HEAD_SPLIT)
         prepare(0, 0, HALF, HALF, HEAD_SPLIT)
+        nc.vector.memset(r8s_rest[:].bitcast(I32), 0)
+        nc.vector.memset(b_rows[:], 0.0)
+        load_scales(nc.gpsimd, r8s_rest, r8_scales, 1, G, R8_ROW)
+        load_bias(nc.gpsimd)
         acc = [bank(m) for m in range(MT)]
         for c0 in (0, QUARTER):
             for m in range(MT):

@@ -94,7 +94,6 @@ def tile_mix_resid_fm_silu_kernel(tc, x, w4_words, w4_scales, r8_words, r8_scale
 
         load_x(0, 0, HALF)
         load_scales(nc.sync, w4s_first, w4_scales, 0, 1, 0)
-        load_scales(nc.gpsimd, w4s_rest, w4_scales, 1, G, 0)
         load_w4(0)
         load_x(0, HALF, HALF)
         load_r8(0, 0, M // 2)
@@ -104,6 +103,8 @@ def tile_mix_resid_fm_silu_kernel(tc, x, w4_words, w4_scales, r8_words, r8_scale
         load_x(0, TW + HALF, HALF)
         for g in range(1, G):
             load_x(g, TW, TW)
+            if g == 1:
+                load_scales(nc.sync, w4s_rest, w4_scales, 1, G, 0)
             load_w4(g)
             load_r8(g)
         for g in range(G):
@@ -231,7 +232,8 @@ def tile_mix_resid_fm_silu_kernel(tc, x, w4_words, w4_scales, r8_words, r8_scale
             mm_w4(acc[m], m, 2, 1)
         for m in range(MT):
             mm_r8(acc[m], m, 2, 1, stop=True)
-            silu(pair[m][:, :TW], acc[m][:], m)
+            at = 0 if m < MT - HELD else TW
+            silu(pair[m][:, at : at + TW], acc[m][:], m)
             if m < MT // 2:
                 mm_w4(acc[m + MT // 2], m + MT // 2, 2, 1)
 
@@ -245,8 +247,6 @@ def tile_mix_resid_fm_silu_kernel(tc, x, w4_words, w4_scales, r8_words, r8_scale
             mm_w4(acc[m], m, 0, 2)
         for m in range(4, MT - HELD):
             both(acc[m], m, 0, 2, start=True)
-        for m in range(MT - HELD, MT):
-            store(pair[m][:, :TW], m, TW, TW)
         prepare(1, 0)
         prepare(2, 0)
         for step in range(MT - HELD + LEAD):
@@ -261,13 +261,18 @@ def tile_mix_resid_fm_silu_kernel(tc, x, w4_words, w4_scales, r8_words, r8_scale
         acc = {}
         for step in range(MT + LEAD_PARKED):
             if step < MT:
-                acc[step] = bank(step + MT - HELD)
-                both(acc[step], step, 1, 0, start=True)
-            m = step - LEAD_PARKED
-            if m >= 0:
+                m = (step + MT - HELD) % MT
+                acc[m] = bank(m)
+                both(acc[m], m, 1, 0, start=True)
+            if step >= LEAD_PARKED:
+                m = (step - LEAD_PARKED + MT - HELD) % MT
                 both(acc[m], m, 2, 0, stop=True)
                 add_parked(acc[m], m, 0)
-                finish(parked[0, m], m, 0)
+                if m < MT - HELD:
+                    finish(parked[0, m], m, 0)
+                else:
+                    silu(pair[m][:, :TW], parked[0, m][:], m)
+                    store(pair[m][:], m, 0, 2 * TW)
         for m in range(MT - HELD, MT - 1):
             one = bank(m)
             for g in range(G):

@@ -89,11 +89,21 @@ def tile_mix_resid_fm_silu_kernel(tc, x, w4_words, w4_scales, r8_words, r8_scale
                     out=view[row0 + r : P : 32, :].rearrange("p (g n) -> p g n", g=g1 - g0), in_=rows[r][:, g0:g1, :]
                 )
 
+        def load_later_r8_scales(q0, q1):
+            view = r8s_rest[:].bitcast(I32)
+            nc.vector.memset(view[32 * q0 : 32 * q1, :], 0)
+            for q in range(q0, q1):
+                nc.gpsimd.dma_start(
+                    out=view[32 * q + R8_ROW : 32 * q + R8_ROW + 4, :].rearrange("p (g n) -> p g n", g=G - 1),
+                    in_=r8_scales.bitcast(I32)[1:, 4 * q : 4 * q + 4, :].rearrange("g r n -> r g n"),
+                )
+
         def load_bias(queue):
             queue.dma_start(out=b_rows[0:P:4, :], in_=b.rearrange("(m q j) -> q m j", q=4, j=32))
 
         load_x(0, 0, HALF)
         load_scales(nc.sync, w4s_first, w4_scales, 0, 1, 0)
+        load_later_r8_scales(0, 2)
         load_w4(0)
         load_x(0, HALF, HALF)
         load_r8(0, 0, M // 2)
@@ -191,10 +201,7 @@ def tile_mix_resid_fm_silu_kernel(tc, x, w4_words, w4_scales, r8_words, r8_scale
 
         prepare(0, 0, 0, HALF, HEAD_SPLIT)
         prepare(0, 0, HALF, HALF, HEAD_SPLIT)
-        nc.vector.memset(r8s_rest[:].bitcast(I32), 0)
-        nc.vector.memset(b_rows[:], 0.0)
-        load_scales(nc.gpsimd, r8s_rest, r8_scales, 1, G, R8_ROW)
-        load_bias(nc.gpsimd)
+        load_later_r8_scales(2, 4)
         acc = [bank(m) for m in range(MT)]
         for c0 in (0, QUARTER):
             for m in range(MT):
@@ -209,6 +216,8 @@ def tile_mix_resid_fm_silu_kernel(tc, x, w4_words, w4_scales, r8_words, r8_scale
 
         prepare(0, 1, 0, HALF)
         prepare(0, 1, HALF, HALF)
+        nc.vector.memset(b_rows[:], 0.0)
+        load_bias(nc.gpsimd)
         for m in range(MT - 2, MT):
             nc.vector.tensor_copy(out=parked[0, m][:], in_=acc[m][:])
         prepare(1, 1, 0, TW, SPLIT)

@@ -211,14 +211,16 @@ def tile_mix_resid_fm_silu_kernel(tc, x, w4_words, w4_scales, r8_words, r8_scale
                 mm_w4(acc[m], m, 0, 0, c0, QUARTER)
         for m in range(MT):
             mm_r8(acc[m], m, 0, 0, stop=True)
-            if m < MT - 2:
+            if m == 0:
+                nc.vector.tensor_copy(out=parked[0, m][:], in_=acc[m][:])
+            elif m < MT - 1:
                 park(acc[m], m, 0)
 
         prepare(0, 1, 0, HALF)
         prepare(0, 1, HALF, HALF)
         nc.vector.memset(b_rows[:], 0.0)
         load_bias(nc.gpsimd)
-        for m in range(MT - 2, MT):
+        for m in range(MT - 1, MT):
             nc.vector.tensor_copy(out=parked[0, m][:], in_=acc[m][:])
         prepare(1, 1, 0, TW, SPLIT)
         acc = [bank(m) for m in range(MT)]

from contextlib import ExitStack

import concourse.mybir as mybir

K, M, T = 1536, 1024, 1536
FLOPS = 2 * 2 * K * M * T

F32 = mybir.dt.float32
BF16 = mybir.dt.bfloat16
I32 = mybir.dt.int32
U32 = mybir.dt.uint32
U8 = mybir.dt.uint8
FP8X4 = mybir.dt.float8_e4m3fn_x4
FP4X4 = mybir.dt.float4_e2m1fn_x4
ACT = mybir.ActivationFunctionType
ALU = mybir.AluOpType

P = 128
PACK = 4
G = K // 512
MT = M // 128
TW = 512
NT = T // TW
HALF = 256
QUARTER = 128
R8_ROW = 4
HEAD_SPLIT = 176
SPLIT = 320
LEAD = 3
LEAD_PARKED = 2
HELD = 2
PARKED = [(0, m) for m in range(MT)]


def tile_mix_resid_fm_silu_kernel(tc, x, w4_words, w4_scales, r8_words, r8_scales, b, out):
    nc = tc.nc
    with ExitStack() as ctx:
        keep = ctx.enter_context(tc.tile_pool(name="keep", bufs=1))
        stage = ctx.enter_context(tc.tile_pool(name="stage", bufs=3))
        outs = ctx.enter_context(tc.tile_pool(name="outs", bufs=12))
        psum = ctx.enter_context(tc.psum_pool(name="psum", bufs=1))
        ctx.enter_context(tc.manual_schedule())

        raw = {}
        codes = {}
        planes = {}
        for t in range(NT):
            for g in range(G):
                codes[g, t] = keep.tile([P, TW], U32, name="codes_%d_%d" % (g, t), align_bytes=256)
                planes[g, t] = keep.tile([P, TW], U8, name="plane_%d_%d" % (g, t), align_bytes=256)
        w4 = [keep.tile([P, 2 * M], U8, name="w4_%d" % g, align_bytes=256) for g in range(G)]
        r8 = [keep.tile([P, 4 * M], U8, name="r8_%d" % g, align_bytes=256) for g in range(G)]
        w4s_first = keep.tile([P, M], U8, name="w4s_first", align_bytes=256)
        r8s_first = keep.tile([P, M], U8, name="r8s_first", align_bytes=256)
        w4s_rest = keep.tile([P, (G - 1) * M], U8, name="w4s_rest", align_bytes=256)
        r8s_rest = keep.tile([P, (G - 1) * M], U8, name="r8s_rest", align_bytes=256)
        parked = {
            (t, m): keep.tile([P, TW], F32, name="parked_%d_%d" % (t, m), align_bytes=64)
            for t, m in PARKED
        }
        pair = [keep.tile([P, 2 * TW], F32, name="pair_%d" % m, align_bytes=64) for m in range(MT)]
        b_rows = keep.tile([P, 32], F32, name="b_rows", align_bytes=64)
        b_cols = keep.tile([P, 32], F32, name="b_cols", align_bytes=64)

        nc.vector.memset(w4s_first[:].bitcast(I32), 0)
        nc.vector.memset(r8s_first[:].bitcast(I32), 0)
        nc.vector.memset(w4s_rest[:].bitcast(I32), 0)

        def load_x(g, c0, width):
            tile = keep.tile([P, PACK, width], F32, name="raw_%d_%d" % (g, c0), align_bytes=64)
            nc.sync.dma_start(
                out=tile[:], in_=x[512 * g : 512 * (g + 1), c0 : c0 + width].rearrange("(p j) t -> p j t", j=PACK)
            )
            for lo in range(0, width, QUARTER):
                raw[g, c0 + lo] = (tile, lo)

        def load_w4(g):
            nc.sync.dma_start(out=w4[g][:].bitcast(I32), in_=w4_words[g].bitcast(I32))

        def load_r8(g, n0=0, n1=M):
            words = r8_words[g].rearrange("p n i -> p (n i)").bitcast(I32)
            nc.sync.dma_start(out=r8[g][:].bitcast(I32)[:, n0:n1], in_=words[:, n0:n1])

        def load_scales(queue, tile, scales, g0, g1, row0):
            rows = scales.bitcast(I32).rearrange("g (q r) n -> r q g n", r=4)
            view = tile[:].bitcast(I32)
            for r in range(4):
                queue.dma_start(
                    out=view[row0 + r : P : 32, :].rearrange("p (g n) -> p g n", g=g1 - g0), in_=rows[r][:, g0:g1, :]
                )

        def load_later_r8_scales(q0, q1):
            view = r8s_rest[:].bitcast(I32)
            nc.vector.memset(view[32 * q0 : 32 * q1, :], 0)
            for q in range(q0, q1):
                nc.gpsimd.dma_start(
                    out=view[32 * q + R8_ROW : 32 * q + R8_ROW + 4, :].rearrange("p (g n) -> p g n", g=G - 1),
                    in_=r8_scales.bitcast(I32)[1:, 4 * q : 4 * q + 4, :].rearrange("g r n -> r g n"),
                )

        def load_bias(queue):
            queue.dma_start(out=b_rows[0:P:4, :], in_=b.rearrange("(m q j) -> q m j", q=4, j=32))

        load_x(0, 0, HALF)
        load_scales(nc.sync, w4s_first, w4_scales, 0, 1, 0)
        load_later_r8_scales(0, 2)
        load_w4(0)
        load_x(0, HALF, HALF)
        load_r8(0, 0, M // 2)
        load_scales(nc.sync, r8s_first, r8_scales, 0, 1, R8_ROW)
        load_r8(0, M // 2, M)
        load_x(0, TW, HALF)
        load_x(0, TW + HALF, HALF)
        for g in range(1, G):
            load_x(g, TW, TW)
            if g == 1:
                load_scales(nc.sync, w4s_rest, w4_scales, 1, G, 0)
            load_w4(g)
            load_r8(g)
        for g in range(G):
            load_x(g, 2 * TW, TW)
        for g in range(1, G):
            load_x(g, 0, TW)

        def cast(g, t, c0=0, width=TW, v_cols=None):
            tile, at = raw[g, TW * t + c0]
            source = tile[:, :, at : at + width]
            v_cols = v_cols or width
            grouped = stage.tile([P, width, PACK], BF16, name="grouped", align_bytes=64)
            for lo, hi in ((0, width // 2), (width // 2, v_cols)):
                nc.vector.tensor_copy(out=grouped[:, lo:hi, :], in_=source[:, :, lo:hi].rearrange("p j w -> p w j"))
            if v_cols < width:
                nc.scalar.copy(out=grouped[:, v_cols:, :], in_=source[:, :, v_cols:].rearrange("p j w -> p w j"))
            return grouped

        def quantise(grouped, g, t, c0=0):
            piece = grouped.shape[1] // 2
            for lo in (0, piece):
                cols = slice(c0 + lo, c0 + lo + piece)
                nc.vector.quantize_mx(
                    out=codes[g, t][:, cols].bitcast(FP8X4),
                    scales=planes[g, t][:, cols],
                    in_=grouped[:, lo : lo + piece, :].rearrange("p w j -> p (w j)"),
                )

        def prepare(g, t, c0=0, width=TW, v_cols=None):
            quantise(cast(g, t, c0, width, v_cols), g, t, c0)

        def bank(i):
            return psum.tile([P, TW], F32, name="bank%d" % (i % MT))

        def mm_w4(acc, m, g, t, c0=0, width=TW, start=False, stop=False):
            scale = w4s_first if g == 0 else w4s_rest
            s0 = M * max(g - 1, 0) + P * m
            step = TW if width == TW else QUARTER
            for lo in range(c0, c0 + width, step):
                nc.tensor.matmul_mx(
                    out=acc[:, lo : lo + step],
                    lhsT=w4[g][:, 256 * m : 256 * (m + 1)].bitcast(FP4X4),
                    lhsT_scale=scale[:, s0 : s0 + P],
                    rhs=codes[g, t][:, lo : lo + step].bitcast(FP8X4),
                    rhs_scale=planes[g, t][:, lo : lo + step],
                    start=(start and lo == c0),
                    stop=(stop and lo + step == c0 + width),
                )

        def mm_r8(acc, m, g, t, c0=0, width=TW, start=False, stop=False):
            scale = r8s_first if g == 0 else r8s_rest
            s0 = M * max(g - 1, 0) + P * m
            nc.tensor.matmul_mx(
                out=acc[:, c0 : c0 + width],
                lhsT=r8[g][:, 512 * m : 512 * (m + 1)].bitcast(FP8X4),
                lhsT_scale=scale[R8_ROW:, s0 : s0 + P],
                rhs=codes[g, t][:, c0 : c0 + width].bitcast(FP8X4),
                rhs_scale=planes[g, t][:, c0 : c0 + width],
                start=start,
                stop=stop,
            )

        def both(acc, m, g, t, start=False, stop=False):
            mm_w4(acc, m, g, t, start=start)
            mm_r8(acc, m, g, t, stop=stop)

        def park(acc, m, t):
            nc.scalar.copy(out=parked[t, m][:], in_=acc[:])

        def silu(target, source, m):
            nc.scalar.activation(out=target, in_=source, func=ACT.Silu, bias=b_cols[:, 4 * m : 4 * m + 1])

        def add_parked(acc, m, t, c0=0, width=TW):
            cols = slice(c0, c0 + width)
            nc.vector.tensor_tensor(out=parked[t, m][:, cols], in0=acc[:, cols], in1=parked[t, m][:, cols], op=ALU.add)

        def store(source, m, c0, width):
            nc.sync.dma_start(out=out[P * m : P * (m + 1), c0 : c0 + width], in_=source)

        def finish(source, m, t, c0=0, width=TW):
            res = outs.tile([P, width], F32, name="res")
            silu(res[:], source[:, c0 : c0 + width], m)
            store(res[:], m, TW * t + c0, width)

        prepare(0, 0, 0, HALF, HEAD_SPLIT)
        prepare(0, 0, HALF, HALF, HEAD_SPLIT)
        load_later_r8_scales(2, 4)
        acc = [bank(m) for m in range(MT)]
        for c0 in (0, QUARTER):
            for m in range(MT):
                mm_w4(acc[m], m, 0, 0, c0, QUARTER, start=(c0 == 0))
        for c0 in (HALF, HALF + QUARTER):
            for m in range(8):
                mm_w4(acc[m], m, 0, 0, c0, QUARTER)
        for m in range(MT):
            mm_r8(acc[m], m, 0, 0, stop=True)
            if m == 0:
                nc.vector.tensor_copy(out=parked[0, m][:], in_=acc[m][:])
            elif m < MT - 1:
                park(acc[m], m, 0)

        prepare(0, 1, 0, HALF)
        prepare(0, 1, HALF, HALF)
        nc.vector.memset(b_rows[:], 0.0)
        load_bias(nc.gpsimd)
        for m in range(MT - 1, MT):
            nc.vector.tensor_copy(out=parked[0, m][:], in_=acc[m][:])
        prepare(1, 1, 0, TW, SPLIT)
        acc = [bank(m) for m in range(MT)]
        for c0 in (0, HALF):
            for m in range(4):
                if m < 4:
                    mm_w4(acc[m], m, 0, 1, c0, HALF, start=(c0 == 0))
                mm_r8(acc[m], m, 0, 1, c0, HALF, start=(c0 == 0 and m >= 4))
        for m in range(4, MT):
            both(acc[m], m, 0, 1, start=True)
        prepare(2, 1, 0, TW, SPLIT)
        nc.vector.transpose(out=b_cols[:], in_=b_rows[:])
        for m in range(MT):
            mm_w4(acc[m], m, 1, 1)
        for m in range(MT):
            mm_r8(acc[m], m, 1, 1)
        prepare(0, 2, 0, HALF)
        prepare(0, 2, HALF, HALF)
        for m in range(MT // 2):
            mm_w4(acc[m], m, 2, 1)
        for m in range(MT):
            mm_r8(acc[m], m, 2, 1, stop=True)
            at = 0 if m < MT - HELD else TW
            silu(pair[m][:, at : at + TW], acc[m][:], m)
            if m < MT // 2:
                mm_w4(acc[m + MT // 2], m + MT // 2, 2, 1)

        prepare(1, 2, 0, TW, 512)
        prepare(2, 2, 0, TW, 320)
        acc = [bank(m) for m in range(MT - HELD)]
        for c0 in (0, HALF):
            for m in range(4):
                mm_r8(acc[m], m, 0, 2, c0, HALF, start=(c0 == 0))
        for m in range(4):
            mm_w4(acc[m], m, 0, 2)
        for m in range(4, MT - HELD):
            both(acc[m], m, 0, 2, start=True)
        prepare(1, 0)
        prepare(2, 0)
        for step in range(MT - HELD + LEAD):
            if step < MT - HELD:
                both(acc[step], step, 1, 2)
            m = step - LEAD
            if m >= 0:
                both(acc[m], m, 2, 2, stop=True)
                silu(pair[m][:, TW:], acc[m][:], m)
                store(pair[m][:], m, TW, 2 * TW)

        acc = {}
        for step in range(MT + LEAD_PARKED):
            if step < MT:
                m = (step + MT - HELD) % MT
                acc[m] = bank(m)
                both(acc[m], m, 1, 0, start=True)
            if step >= LEAD_PARKED:
                m = (step - LEAD_PARKED + MT - HELD) % MT
                both(acc[m], m, 2, 0, stop=True)
                add_parked(acc[m], m, 0)
                if m < MT - HELD:
                    finish(parked[0, m], m, 0)
                else:
                    silu(pair[m][:, :TW], parked[0, m][:], m)
                    store(pair[m][:], m, 0, 2 * TW)
        for m in range(MT - HELD, MT - 1):
            one = bank(m)
            for g in range(G):
                both(one, m, g, 2, start=(g == 0), stop=(g == G - 1))
            finish(one, m, 2)
        m = MT - 1
        for i, (c0, width) in enumerate(((0, HALF), (HALF, QUARTER), (HALF + QUARTER, QUARTER))):
            last = bank(m + i)
            for g in range(G):
                mm_w4(last, m, g, 2, c0, width, start=(g == 0))
                mm_r8(last, m, g, 2, c0, width, stop=(g == G - 1))
            finish(last, m, 2, c0, width)
